import numpy as np
import ml_dtypes


def mxq(x, axis, fmt="e4m3"):
    dtype, down = {"e4m3": (ml_dtypes.float8_e4m3fn, 7), "e5m2": (ml_dtypes.float8_e5m2, 14)}[fmt]
    v = np.moveaxis(np.asarray(x, np.float32).astype(ml_dtypes.bfloat16).astype(np.float64), axis, -1)
    blocks = v.reshape(v.shape[:-1] + (-1, 32))
    amax = np.abs(blocks).max(-1, keepdims=True)
    byte = np.maximum(np.where(amax > 0, np.frexp(amax)[1] - 1 + 127, 0) - down, 1)
    scale = np.exp2(byte - 127.0)
    codes = (blocks / scale).astype(np.float32).astype(dtype).astype(np.float64)
    return np.moveaxis((codes * scale).reshape(v.shape), -1, axis)


WIDE = False


def mx_kscale(k):
    if not WIDE:
        return np.ones(k)
    levels = np.array([10, -10, 5, -5, 0])
    if k % 512:
        return np.exp2(np.random.permutation(np.resize(levels, k // 32))).repeat(32)
    a = np.empty((k // 512, 16))
    for p in range(k // 512):
        a[p, :8] = np.random.permutation(np.resize(levels, 8))
        for g in range(8):
            far = levels[np.abs(levels - a[p, g]) >= 10]
            a[p, g + 8] = far[np.random.randint(len(far))]
    return np.exp2(a.ravel()).repeat(32)


BF16 = ml_dtypes.bfloat16


def bf(x):
    return np.asarray(x, np.float32).astype(BF16)


def f64(x):
    return np.asarray(x).astype(np.float64)


E2M1 = np.array([0.0, 0.5, 1.0, 1.5, 2.0, 3.0, 4.0, 6.0, -0.0, -0.5, -1.0, -1.5, -2.0, -3.0, -4.0, -6.0])


def pack_weight(w, fmt):
    k, n = w.shape
    w = f64(bf(w)).reshape(k // 32, 32, n)
    amax = np.abs(w).max(1)
    if fmt == "e4m3":
        byte = np.frexp(amax)[1] - 1 + 127 - 7
    else:
        mant, ex = np.frexp(amax / 6.0)
        byte = np.where(mant > 0.5, ex, ex - 1) + 127
    byte = np.clip(np.where(amax > 0, byte, 1), 1, 254)
    scaled = (w * np.exp2(127.0 - byte)[:, None, :]).reshape(k, n).astype(np.float32)
    by_word = np.ascontiguousarray(scaled.reshape(k // 512, 128, 4, n).transpose(0, 1, 3, 2))
    if fmt == "e4m3":
        words = by_word.astype(ml_dtypes.float8_e4m3fn).view(np.uint8)
    else:
        c = by_word.astype(ml_dtypes.float4_e2m1fn).view(np.uint8) & 0xF
        words = c[..., 0::2] | (c[..., 1::2] << 4)
    return np.ascontiguousarray(words), np.ascontiguousarray(byte.astype(np.uint8).reshape(k // 512, 16, n))


def unpack_weight(words, scales, fmt):
    g, p, n, _ = words.shape
    if fmt == "e4m3":
        vals = np.ascontiguousarray(words).view(ml_dtypes.float8_e4m3fn).astype(np.float64)
    else:
        nib = np.empty((g, p, n, 4), np.uint8)
        nib[..., 0::2] = words & 0xF
        nib[..., 1::2] = words >> 4
        vals = E2M1[nib]
    vals = vals * np.repeat(np.exp2(scales.astype(np.float64) - 127.0), 8, axis=1)[..., None]
    return vals.transpose(0, 1, 3, 2).reshape(g * 512, n)

E4M3FN = np.array([(-1.0 if i & 128 else 1.0) * ((1.0 + (i & 7) / 8.0) * 2.0 ** (((i >> 3) & 15) - 7) if i & 120 else (i & 7) * 2.0 ** -9) for i in range(256)])


def e4m3fn_bytes(y):
    return np.clip(np.asarray(y, np.float64), -448.0, 448.0).astype(np.float32).astype(ml_dtypes.float8_e4m3fn).view(np.uint8)


def e4m3fn_values(b):
    return E4M3FN[b]


T, D, C, H = 1024, 1024, 512, 512
E = 2 * C


def sigmoid(v):
    return 1.0 / (1.0 + np.exp(-v))


def softplus(v):
    return np.maximum(v, 0.0) + np.log1p(np.exp(-np.abs(v)))


def _interval_mass(d, sc):
    upper = sigmoid((0.5 - d) / sc)
    lower = sigmoid((-0.5 - d) / sc)
    return upper - lower


def draw0():
    s, t, r = mx_kscale(D), mx_kscale(C), mx_kscale(H)
    x = bf(np.random.standard_normal((T, D)) * s)
    wa_words, wa_scales = pack_weight(np.random.standard_normal((D, E)) / np.sqrt(D) / s[:, None], "e4m3")
    u = bf(np.random.uniform(-0.5, 0.5, (T, E)))
    g = bf(np.random.uniform(0.5, 1.5, C) * t)
    wctx_words, wctx_scales = pack_weight(np.random.standard_normal((C, E)) / np.sqrt(C) / t[:, None], "e4m3")
    z = bf(np.random.standard_normal((T, H)) * r)
    wz_words, wz_scales = pack_weight(np.random.standard_normal((H, C)) * 2.0 / np.sqrt(H) / r[:, None], "e4m3")
    return {
        "x": x,
        "wa_words": wa_words,
        "wa_scales": wa_scales,
        "u": u,
        "g": g,
        "wctx_words": wctx_words,
        "wctx_scales": wctx_scales,
        "z": z,
        "wz_words": wz_words,
        "wz_scales": wz_scales,
    }


def core(x, wa_words, wa_scales, u, g, wctx_words, wctx_scales, z, wz_words, wz_scales):
    c = g.shape[0]
    y = (mxq(f64(x), 1, "e4m3") @ unpack_weight(wa_words, wa_scales, "e4m3")) + f64(u)
    y1 = y[:, :c]
    y2 = y[:, c:]
    k = mxq(y1 * f64(g)[None, :], 1, "e4m3") @ unpack_weight(wctx_words, wctx_scales, "e4m3")
    mu = k[:, :c] + (mxq(f64(z), 1, "e4m3") @ unpack_weight(wz_words, wz_scales, "e4m3"))
    sc = 0.3 + 0.5 * softplus(k[:, c:])
    d = np.abs(y2 - mu)
    p = _interval_mass(d, sc)
    return -np.log(np.maximum(p, 1e-6)) / np.log(2.0)


def setup_inputs():
    drawn = draw0()
    full = np.asarray(drawn['x']).astype(np.float64)
    scale = (np.abs(full).reshape(1024, 8, 128).max(axis=(2,)) / 448.0).astype(np.float32)
    given = {}
    for key, value in drawn.items():
        if key == 'x':
            given['x_bytes'] = e4m3fn_bytes(full / np.repeat(scale.astype(np.float64), 128, axis=1))
            given['x_scale'] = scale
        else:
            given[key] = value
    return given


def reference(x_bytes, x_scale, wa_words, wa_scales, u, g, wctx_words, wctx_scales, z, wz_words, wz_scales):
    return core(e4m3fn_values(x_bytes) * np.repeat(x_scale.astype(np.float64), 128, axis=1), wa_words, wa_scales, u, g, wctx_words, wctx_scales, z, wz_words, wz_scales)

@@ -1,0 +1,278 @@
+import math
+from contextlib import ExitStack
+
+import concourse.mybir as mybir
+from concourse.masks import make_identity
+
+T, D, C, H = 1024, 1024, 512, 512
+E = 2 * C
+FLOPS = 2 * T * (D * E + C * E + H * C)
+
+F32 = mybir.dt.float32
+BF16 = mybir.dt.bfloat16
+U32 = mybir.dt.uint32
+I32 = mybir.dt.int32
+U8 = mybir.dt.uint8
+FP8 = mybir.dt.float8_e4m3fn
+FP8X4 = mybir.dt.float8_e4m3fn_x4
+ALU = mybir.AluOpType
+ACT = mybir.ActivationFunctionType
+
+P = 128
+TILES = T // P
+PAIRS = TILES // 2
+BLK = 128
+LN_GUARD = 2.0**-63
+P_FLOOR = 1e-6
+
+ORDER = """
+W.5.P XA.0.A XB.0.V XA.1.V XB.1.V XT.0.0 W.1.P XB.2.A XT.1.1 W.1.P XA.2.V XC.0.A
+XB.3.V XA.3.V XT.2.2 W.1.P XC.1.A XC.2.A XQ.0.V XQ.1.V XT.3.3 XB.4.V Y1.0.4 Y1.1.5
+XA.4.A XT.4.6 XC.3.A XQ.2.V E1.0.V XA.5.A YT.0.7 XC.4.A Y1.2.0 XB.5.A XA.6.A E1.1.V
+XB.6.A XQ.3.V GX.0.V E2.0.V Y1.3.1 XA.7.A YT.1.2 XT.5.3 XQ.4.V E1.2.V YT.2.4 Y1.4.5
+XC.5.A E2.1.V YQ.0.V E1.3.V KC.0.6 XB.7.A E1.4.V SG.0.A XQ.5.V XT.6.7 E2.2.V YQ.1.V
+YT.3.0 XC.6.A YQ.2.V YT.4.2 E2.3.V Y1.5.1 KC.1.3 E2.4.V XT.7.5 XQ.6.V ZT.0.4 E1.5.V
+KC.2.7 YQ.3.V VE.0.A XC.7.A SG.1.A XQ.7.V Y1.6.0 ZC.0.A E1.6.V YT.5.6 KC.3.2 E2.5.V
+YQ.4.V Y1.7.5 E1.7.V YT.6.1 SG.2.A E2.6.V ZT.1.4 YQ.5.V VE.1.A YT.7.0 YQ.6.V E2.7.V
+KC.4.6 KC.5.3 YQ.7.V KC.6.5 ZT.2.1 ZQ.0.V SG.3.A ZC.1.A SG.4.A KC.7.4 SG.5.A D.0.0
+ZQ.1.V ZC.2.V DE.0.V D.1.1 ZT.3.0 SG.6.A ZQ.2.V DE.1.V AB.0.V SG.7.A ZC.3.V LA.0.A
+D.2.1 LA.1.A MN.0.V MN.1.V LA.2.A MN.2.V MN.3.V LA.3.A MN.4.V LB.0.A D.3.0 D.4.7
+D.5.2 ZQ.3.V MN.5.V LB.1.A D.6.6 MN.6.V LB.2.A MN.7.V DE.2.V DE.3.V D.7.3 DE.4.V
+LB.3.A DE.5.V AB.1.V H.0.A DE.6.V H.1.A H.2.A DE.7.V M2.0.V H.3.A M1.0.V M2.1.V
+AB.2.A M1.1.V SS.0.A M2.2.V M1.2.V AB.3.V SS.1.A SS.2.A M2.3.V M1.3.V P.0.V SS.3.A
+P.1.V LP.0.A P.2.V P.3.V LP.1.A LP.2.A FN.0.V FN.1.V LP.3.A FN.2.V FN.3.V LP.4.A
+LP.5.A FN.4.V LP.6.A FN.5.V FN.6.V LP.7.A FN.7.V
+"""
+
+
+def tile_channelconditionalsliceratemap_d1p_kernel(
+    tc, x_bytes, x_scale, wa_words, wa_scales, u, g, wctx_words, wctx_scales, z, wz_words, wz_scales, out
+):
+    nc = tc.nc
+    x_rows = x_bytes.rearrange("(p i) k -> p i k", i=TILES)
+    u_rows = u.rearrange("(p i) e -> p i e", i=TILES)
+    z_rows = z.rearrange("(p i) k -> p i k", i=TILES)
+    out_rows = out.rearrange("(p i) c -> p i c", i=TILES)
+
+    with ExitStack() as ctx:
+        keep = ctx.enter_context(tc.tile_pool(name="keep", bufs=1))
+        work = ctx.enter_context(tc.tile_pool(name="work", bufs=8))
+        psum = ctx.enter_context(tc.psum_pool(name="psum", bufs=1))
+        ctx.enter_context(tc.manual_schedule())
+
+        def kept(name, shape, dtype):
+            return keep.tile(shape, dtype, name=name, align_bytes=64)
+
+        def rotating(name, shape, dtype, bufs=8):
+            return work.tile(shape, dtype, name=name, align_bytes=64, bufs=bufs)
+
+        def bank(b, shape):
+            return psum.tile(shape, F32, name="bank%d" % b)
+
+        wa_sc = kept("wa_sc", [P, 2, E], U8)
+        wctx_sc = kept("wctx_sc", [P, 1, E], U8)
+        wz_sc = kept("wz_sc", [P, 1, C], U8)
+        warm = kept("warm", [P, 1], F32)
+        warm_out = kept("warm_out", [P, 1], F32)
+        ident = kept("ident", [P, P], F32)
+        zeros = kept("zeros", [P, C], BF16)
+        guard = kept("guard", [P, 1], F32)
+        one = kept("one", [P, 1], F32)
+        nc.gpsimd.memset(wa_sc[:].bitcast(I32), 0)
+        make_identity(nc, ident[:])
+        nc.gpsimd.memset(wctx_sc[:].bitcast(I32), 0)
+        nc.gpsimd.memset(wz_sc[:].bitcast(I32), 0)
+        nc.vector.memset(warm[:], 0.0)
+        nc.vector.memset(zeros[:].bitcast(I32), 0)
+        nc.vector.memset(guard[:], LN_GUARD)
+        nc.vector.memset(one[:], 1.0)
+
+        def load_scales(queue, plane, scales):
+            rows = scales.bitcast(I32).rearrange("g (q r) n -> r q g n", r=4)
+            for r in range(4):
+                queue.dma_start(out=plane[r:P:32].bitcast(I32), in_=rows[r])
+
+        def load_words(name, words, half):
+            passes = words.shape[0]
+            tile = kept(name, [P, passes, C], U32)
+            src = words.rearrange("g p n t -> p g (n t)")[:, :, 4 * C * half : 4 * C * (half + 1)]
+            nc.sync.dma_start(out=tile[:].bitcast(I32), in_=src.bitcast(I32))
+            return tile
+
+        def load_rows(name, rows, first, count, dtype):
+            tile = kept(name, [P, count, rows.shape[2]], dtype)
+            nc.sync.dma_start(out=tile[:], in_=rows[:, first : first + count, :])
+            return [tile[:, n, :] for n in range(count)]
+
+        load_scales(nc.scalar, wa_sc, wa_scales)
+        nc.scalar.activation(out=warm_out[:], in_=warm[:], func=ACT.Sigmoid)
+
+        xs = kept("xs", [P, TILES * 8], F32)
+        nc.sync.dma_start(out=xs[:], in_=x_scale.rearrange("(p i) j -> p (i j)", i=TILES))
+        xraw = load_rows("xraw0", x_rows, 0, 1, U8)
+        xraw = xraw + load_rows("xraw1", x_rows, 1, 1, U8)
+        xraw = xraw + load_rows("xraw2", x_rows, 2, 2, U8)
+        wa1 = load_words("wa1", wa_words, 0)
+        xraw = xraw + load_rows("xraw4", x_rows, 4, 2, U8)
+        u1 = load_rows("u1a", u_rows[:, :, 0:C], 0, 2, BF16)
+        g4 = kept("g4", [P, 4], BF16)
+        nc.sync.dma_start(out=g4[:], in_=g.rearrange("(p t) -> p t", t=4))
+        xraw = xraw + load_rows("xraw6", x_rows, 6, 2, U8)
+        u1 = u1 + load_rows("u1b", u_rows[:, :, 0:C], 2, 2, BF16)
+        load_scales(nc.sync, wctx_sc, wctx_scales)
+        wsc = load_words("wsc", wctx_words, 1)
+        u1 = u1 + load_rows("u1c", u_rows[:, :, 0:C], 4, 4, BF16)
+        zraw = load_rows("zrawa", z_rows, 0, 4, BF16)
+        zraw = zraw + load_rows("zrawb", z_rows, 4, 4, BF16)
+        load_scales(nc.sync, wz_sc, wz_scales)
+        wz = load_words("wz", wz_words, 0)
+        wa2 = load_words("wa2", wa_words, 1)
+        wmu = load_words("wmu", wctx_words, 0)
+        u2 = load_rows("u2a", u_rows[:, :, C:E], 0, 4, BF16)
+        u2 = u2 + load_rows("u2b", u_rows[:, :, C:E], 4, 4, BF16)
+
+        nxs = kept("nxs", [P, TILES * 8], F32)
+        nc.vector.tensor_scalar(out=nxs[:], in0=xs[:], scalar1=-1.0, scalar2=None, op0=ALU.mult)
+        gx = kept("gx", [P, P, 4], BF16)
+
+        xcode = [kept("xcode%d" % i, [P, 2, P], U32) for i in range(TILES)]
+        xsc = [kept("xsc%d" % i, [P, 2, P], U8) for i in range(TILES)]
+        ycode = [kept("ycode%d" % i, [P, P], U32) for i in range(TILES)]
+        ysc = [kept("ysc%d" % i, [P, P], U8) for i in range(TILES)]
+        zcode = [kept("zcode%d" % j, [P, 2, P], U32) for j in range(PAIRS)]
+        zsc = [kept("zsc%d" % j, [P, 2, P], U8) for j in range(PAIRS)]
+        sg = [kept("sg%d" % j, [P, 2 * C], F32) for j in range(PAIRS)]
+        nsp = [kept("nsp%d" % j, [P, 2 * C], F32) for j in range(PAIRS)]
+        dl = [kept("dl%d" % j, [P, 2 * C], F32) for j in range(PAIRS)]
+        mm = [kept("mm%d" % j, [P, 4 * C], F32) for j in range(PAIRS)]
+        pp = sg
+        t = {}
+
+        def half(tiles, i):
+            return tiles[i // 2][:, C * (i % 2) : C * (i % 2 + 1)]
+
+        def pieces(i):
+            return [slice(0, C)] if i < TILES - 1 else [slice(0, C // 2), slice(C // 2, C)]
+
+        def copy(eng, dst, src):
+            if eng == "A":
+                nc.scalar.copy(out=dst, in_=src)
+            else:
+                nc.vector.tensor_copy(out=dst, in_=src)
+
+        def widen(i, g_pass, eng):
+            if ("xb", i) not in t:
+                t["xb", i] = rotating("xb", [P, D], BF16)
+            for j in range(4 * g_pass, 4 * g_pass + 4):
+                cols = slice(BLK * j, BLK * (j + 1))
+                src = xraw[i][:, cols].bitcast(FP8)
+                s = nxs[:, 8 * i + j : 8 * i + j + 1]
+                if eng == "A":
+                    nc.scalar.activation(out=t["xb", i][:, cols], in_=src, func=ACT.Copy, scale=s)
+                else:
+                    nc.vector.tensor_scalar(out=t["xb", i][:, cols], in0=src, scalar1=s, scalar2=None, op0=ALU.mult)
+
+        def turn(dst, rows):
+            words = rows.bitcast(F32)
+            for w in (0, 1):
+                nc.tensor.transpose(dst[:, w, :], words[:, w : 256 : 2], ident[:])
+
+        def mx(acc, lc, ls, rc, rs, start, stop):
+            nc.tensor.matmul_mx(out=acc, lhsT=lc.bitcast(FP8X4), lhsT_scale=ls, rhs=rc.bitcast(FP8X4), rhs_scale=rs, start=start, stop=stop)
+
+        def step(st, i, arg):
+            if st == "W":
+                if "warm" not in t:
+                    t["warm"] = bank(7, [P, C])
+                for n in range(i):
+                    nc.tensor.matmul(t["warm"][:], lhsT=zeros[:, 0:P], rhs=zeros[:], start=True, stop=True)
+            elif st == "GX":
+                nc.vector.tensor_copy(out=gx[:], in_=g4[:].unsqueeze(1).to_broadcast([P, P, 4]))
+            elif st == "XA":
+                widen(i, 0, arg)
+            elif st == "XB":
+                widen(i, 1, arg)
+            elif st == "XT":
+                t["pA", i] = bank(int(arg), [P, 2, 2, P])
+                for gp in (0, 1):
+                    turn(t["pA", i][:, gp], t["xb", i][:, 512 * gp : 512 * (gp + 1)])
+            elif st == "XC":
+                t["xg", i] = rotating("xg", [P, D], BF16)
+                copy(arg, t["xg", i][:].bitcast(F32).rearrange("p (g r w) -> p g r w", g=2, w=2), t["pA", i][:].rearrange("p g w r -> p g r w"))
+            elif st == "XQ":
+                nc.vector.quantize_mx(out=xcode[i][:].rearrange("p g r -> p (g r)").bitcast(FP8X4), scales=xsc[i][:].rearrange("p g r -> p (g r)"), in_=t["xg", i][:])
+            elif st == "Y1":
+                t["pB", i] = bank(int(arg), [P, C])
+                for gp in (0, 1):
+                    mx(t["pB", i][:], xcode[i][:, gp, :], xsc[i][:, gp, :], wa1[:, gp, :], wa_sc[:, gp, 0:C], gp == 0, gp == 1)
+            elif st == "E1":
+                t["y1", i] = rotating("y1", [P, 4, P], F32)
+                nc.vector.tensor_tensor(out=t["y1", i][:], in0=u1[i].rearrange("p (m t) -> p t m", t=4), in1=t["pB", i][:].rearrange("p (m t) -> p t m", t=4), op=ALU.subtract)
+            elif st == "YT":
+                t["pC", i] = bank(int(arg), [P, 4, P])
+                for k in range(4):
+                    nc.tensor.transpose(t["pC", i][:, k, :], t["y1", i][:, k, :], ident[:])
+            elif st == "E2":
+                t["yg", i] = rotating("yg", [P, P, 4], BF16)
+                nc.vector.tensor_tensor(out=t["yg", i][:], in0=t["pC", i][:].rearrange("p t r -> p r t"), in1=gx[:], op=ALU.mult)
+            elif st == "YQ":
+                nc.vector.quantize_mx(out=ycode[i][:].bitcast(FP8X4), scales=ysc[i][:], in_=t["yg", i][:].rearrange("p r t -> p (r t)"))
+            elif st == "KC":
+                t["pV", i] = bank(int(arg), [P, C])
+                t["v", i] = t["pV", i]
+                mx(t["pV", i][:], ycode[i][:], ysc[i][:], wsc[:, 0, :], wctx_sc[:, 0, C:E], True, True)
+            elif st == "SG":
+                nc.scalar.activation(out=half(sg, i), in_=t["pV", i][:], func=ACT.Sigmoid, scale=-1.0)
+            elif st == "VE":
+                t["v", i] = kept("vs%d" % i, [P, C], F32)
+                copy(arg, t["v", i][:], t["pV", i][:])
+            elif st == "ZT":
+                t["pZ", i] = bank(int(arg), [P, 2, 2, P])
+                for n in (0, 1):
+                    turn(t["pZ", i][:, n], zraw[2 * i + n])
+            elif st == "ZC":
+                t["zg", i] = rotating("zg", [P, D], BF16, 4)
+                copy(arg, t["zg", i][:].bitcast(F32).rearrange("p (g r w) -> p g r w", g=2, w=2), t["pZ", i][:].rearrange("p g w r -> p g r w"))
+            elif st == "ZQ":
+                nc.vector.quantize_mx(out=zcode[i][:].rearrange("p g r -> p (g r)").bitcast(FP8X4), scales=zsc[i][:].rearrange("p g r -> p (g r)"), in_=t["zg", i][:])
+            elif st == "D":
+                t["pD", i] = bank(int(arg), [P, C])
+                acc = t["pD", i][:]
+                for gp in (0, 1):
+                    mx(acc, xcode[i][:, gp, :], xsc[i][:, gp, :], wa2[:, gp, :], wa_sc[:, gp, C:E], gp == 0, False)
+                mx(acc, ycode[i][:], ysc[i][:], wmu[:, 0, :], wctx_sc[:, 0, 0:C], False, False)
+                mx(acc, zcode[i // 2][:, i % 2, :], zsc[i // 2][:, i % 2, :], wz[:, 0, :], wz_sc[:, 0, :], False, True)
+            elif st == "DE":
+                nc.vector.tensor_tensor(out=half(dl, i), in0=t["pD", i][:], in1=u2[i], op=ALU.subtract)
+            elif st == "AB":
+                if arg == "A":
+                    nc.scalar.activation(out=dl[i][:], in_=dl[i][:], func=ACT.Abs)
+                else:
+                    nc.vector.scalar_tensor_tensor(out=dl[i][:], in0=dl[i][:], scalar=-1.0, in1=dl[i][:], op0=ALU.mult, op1=ALU.max)
+            elif st == "LA":
+                nc.scalar.activation(out=sg[i][:], in_=sg[i][:], func=ACT.Ln, bias=guard[:])
+            elif st == "MN":
+                nc.vector.scalar_tensor_tensor(out=half(nsp, i), in0=t["v", i][:], scalar=-1.0, in1=half(sg, i), op0=ALU.mult, op1=ALU.min)
+            elif st == "LB":
+                nc.scalar.activation(out=nsp[i][:], in_=nsp[i][:], func=ACT.Ln, scale=-1.0 / 0.3, bias=one[:])
+            elif st == "H":
+                nc.scalar.activation(out=nsp[i][:], in_=nsp[i][:], func=ACT.Sigmoid, scale=-1.0)
+            elif st == "M1":
+                nc.vector.scalar_tensor_tensor(out=mm[i][:, 0 : 2 * C], in0=dl[i][:], scalar=-0.5, in1=nsp[i][:], op0=ALU.add, op1=ALU.mult)
+            elif st == "M2":
+                nc.vector.scalar_tensor_tensor(out=mm[i][:, 2 * C : 4 * C], in0=dl[i][:], scalar=0.5, in1=nsp[i][:], op0=ALU.add, op1=ALU.mult)
+            elif st == "SS":
+                nc.scalar.activation(out=mm[i][:], in_=mm[i][:], func=ACT.Sigmoid, scale=-1.0 / 0.15)
+            elif st == "P":
+                nc.vector.scalar_tensor_tensor(out=pp[i][:], in0=mm[i][:, 0 : 2 * C], scalar=P_FLOOR, in1=mm[i][:, 2 * C : 4 * C], op0=ALU.max, op1=ALU.subtract)
+            elif st == "LP":
+                for cols in pieces(i):
+                    nc.scalar.activation(out=half(pp, i)[:, cols], in_=half(pp, i)[:, cols], func=ACT.Ln, bias=guard[:])
+            elif st == "FN":
+                for cols in pieces(i):
+                    nc.vector.tensor_scalar(out=half(dl, i)[:, cols], in0=half(pp, i)[:, cols], scalar1=-1.0 / math.log(2.0), scalar2=-math.log(P_FLOOR) / math.log(2.0), op0=ALU.mult, op1=ALU.min)
+                    nc.sync.dma_start(out=out_rows[:, i, cols], in_=half(dl, i)[:, cols])
+
+        for item in ORDER.split():
+            name, i, arg = item.split(".")
+            step(name, int(i), arg)

@@ -19,29 +19,36 @@ ALU = mybir.AluOpType
 ACT = mybir.ActivationFunctionType
 
 P = 128
+PACK = 4
+K_PASS = P * PACK
 TILES = T // P
 PAIRS = TILES // 2
-BLK = 128
+SCALE_SPAN = 128
+SCALES_PER_ROW = D // SCALE_SPAN
 LN_GUARD = 2.0**-63
 P_FLOOR = 1e-6
+WARM_BANK = 7
+HEAD_WARMUPS = 9
 
-ORDER = """
-W.5.P XA.0.A XB.0.V XA.1.V XB.1.V XT.0.0 W.1.P XB.2.A XT.1.1 W.1.P XA.2.V XC.0.A
-XB.3.V XA.3.V XT.2.2 W.1.P XC.1.A XC.2.A XQ.0.V XQ.1.V XT.3.3 XB.4.V Y1.0.4 Y1.1.5
-XA.4.A XT.4.6 XC.3.A XQ.2.V E1.0.V XA.5.A YT.0.7 XC.4.A Y1.2.0 XB.5.A XA.6.A E1.1.V
-XB.6.A XQ.3.V GX.0.V E2.0.V Y1.3.1 XA.7.A YT.1.2 XT.5.3 XQ.4.V E1.2.V YT.2.4 Y1.4.5
-XC.5.A E2.1.V YQ.0.V E1.3.V KC.0.6 XB.7.A E1.4.V SG.0.A XQ.5.V XT.6.7 E2.2.V YQ.1.V
-YT.3.0 XC.6.A YQ.2.V YT.4.2 E2.3.V Y1.5.1 KC.1.3 E2.4.V XT.7.5 XQ.6.V ZT.0.4 E1.5.V
-KC.2.7 YQ.3.V VE.0.A XC.7.A SG.1.A XQ.7.V Y1.6.0 ZC.0.A E1.6.V YT.5.6 KC.3.2 E2.5.V
-YQ.4.V Y1.7.5 E1.7.V YT.6.1 SG.2.A E2.6.V ZT.1.4 YQ.5.V VE.1.A YT.7.0 YQ.6.V E2.7.V
-KC.4.6 KC.5.3 YQ.7.V KC.6.5 ZT.2.1 ZQ.0.V SG.3.A ZC.1.A SG.4.A KC.7.4 SG.5.A D.0.0
-ZQ.1.V ZC.2.V DE.0.V D.1.1 ZT.3.0 SG.6.A ZQ.2.V DE.1.V AB.0.V SG.7.A ZC.3.V LA.0.A
-D.2.1 LA.1.A MN.0.V MN.1.V LA.2.A MN.2.V MN.3.V LA.3.A MN.4.V LB.0.A D.3.0 D.4.7
-D.5.2 ZQ.3.V MN.5.V LB.1.A D.6.6 MN.6.V LB.2.A MN.7.V DE.2.V DE.3.V D.7.3 DE.4.V
-LB.3.A DE.5.V AB.1.V H.0.A DE.6.V H.1.A H.2.A DE.7.V M2.0.V H.3.A M1.0.V M2.1.V
-AB.2.A M1.1.V SS.0.A M2.2.V M1.2.V AB.3.V SS.1.A SS.2.A M2.3.V M1.3.V P.0.V SS.3.A
-P.1.V LP.0.A P.2.V P.3.V LP.1.A LP.2.A FN.0.V FN.1.V LP.3.A FN.2.V FN.3.V LP.4.A
-LP.5.A FN.4.V LP.6.A FN.5.V FN.6.V LP.7.A FN.7.V
+FIRST_SIGMOID_PHASE = """
+widen_lo:0:S widen_hi:0:V widen_hi:1:V widen_lo:1:S turn_x:0:0 warm:1 widen_lo:2:V widen_hi:2:V turn_x:1:1
+warm:1 lay_x:0:S widen_lo:3:V widen_hi:3:V turn_x:2:2 warm:1 lay_x:1:S quant_x:0 turn_x:3:3 quant_x:1
+lay_x:2:S lay_x:3:S widen_hi:4:S quant_x:2 widen_hi:5:S mm_y1:0:4 widen_lo:4:V quant_x:3 mm_y1:1:5
+widen_lo:5:S mm_y1:2:6 mm_y1:3:7 add_u1:0 add_u1:1 turn_y1:0:0 turn_y1:1:1 add_u1:2 spread_g gain:0 add_u1:3
+turn_x:4:2 turn_x:5:3 gain:1 widen_lo:6:S widen_hi:6:S turn_y1:2:4 widen_hi:7:S turn_x:6:5 turn_y1:3:6
+widen_lo:7:S turn_x:7:0 lay_x:4:S quant_y:0 lay_x:5:S lay_x:6:S gain:2 quant_y:1 quant_x:4 mm_v:0:7 mm_v:1:1
+mm_y1:4:4 lay_x:7:S quant_y:2 quant_x:5 mm_y1:5:2 park_v:0:S gain:3 mm_v:2:3 quant_x:6 mm_y1:6:5 quant_y:3
+mm_v:3:6 quant_x:7 add_u1:4 add_u1:5 add_u1:6 mm_y1:7:0 turn_y1:4:4 gain:4 turn_z:0:2 sig_v:0 turn_z:1:7
+turn_y1:5:5 sig_v:1 add_u1:7 quant_y:4 gain:5 turn_y1:6:4 turn_z:2:0 park_v:1:S lay_z:0:S gain:6 lay_z:1:S
+quant_y:5 quant_z:0 sig_v:2 turn_y1:7:1 lay_z:2:S turn_z:3:2 quant_y:6 gain:7 sig_v:3 mm_v:4:7 mm_v:5:5
+lay_z:3:V quant_y:7 quant_z:1 quant_z:2 mm_v:6:4 quant_z:3 mm_diff:0:0 mm_v:7:1 sig_v:4 sig_v:5 sig_v:6
+sig_v:7
+"""
+FIRST_LN_PHASE = """
+mm_diff:1:2 sub_u2:0 sub_u2:1 abs_d:0 mm_diff:2:0 mm_diff:3:2 sub_u2:2 sub_u2:3 mm_diff:4:0 mm_diff:5:2
+ln_sig:0 ln_sig:1 ln_sig:2 ln_sig:3 pick_sp:0 pick_sp:1 pick_sp:2 mm_diff:6:3 sub_u2:4 mm_diff:7:0
+pick_sp:3 pick_sp:4 pick_sp:5 pick_sp:6 pick_sp:7 ln_den:0 ln_den:1 ln_den:2 ln_den:3
+sub_u2:5 sub_u2:6 abs_d:1 sub_u2:7 abs_d:2 abs_d:3
 """
 
 
@@ -55,224 +62,282 @@ def tile_channelconditionalsliceratemap_d1p_kernel(
     out_rows = out.rearrange("(p i) c -> p i c", i=TILES)
 
     with ExitStack() as ctx:
-        keep = ctx.enter_context(tc.tile_pool(name="keep", bufs=1))
-        work = ctx.enter_context(tc.tile_pool(name="work", bufs=8))
+        pool = ctx.enter_context(tc.tile_pool(name="sbuf", bufs=1))
         psum = ctx.enter_context(tc.psum_pool(name="psum", bufs=1))
         ctx.enter_context(tc.manual_schedule())
 
-        def kept(name, shape, dtype):
-            return keep.tile(shape, dtype, name=name, align_bytes=64)
+        def sbuf(name, shape, dtype):
+            return pool.tile(shape, dtype, name=name, align_bytes=64)
 
-        def rotating(name, shape, dtype, bufs=8):
-            return work.tile(shape, dtype, name=name, align_bytes=64, bufs=bufs)
+        def each(name, count, shape, dtype):
+            return [sbuf("%s%d" % (name, n), shape, dtype) for n in range(count)]
 
-        def bank(b, shape):
-            return psum.tile(shape, F32, name="bank%d" % b)
+        def bank(number, shape):
+            return psum.tile(shape, F32, name="bank%s" % number)
 
-        wa_sc = kept("wa_sc", [P, 2, E], U8)
-        wctx_sc = kept("wctx_sc", [P, 1, E], U8)
-        wz_sc = kept("wz_sc", [P, 1, C], U8)
-        warm = kept("warm", [P, 1], F32)
-        warm_out = kept("warm_out", [P, 1], F32)
-        ident = kept("ident", [P, P], F32)
-        zeros = kept("zeros", [P, C], BF16)
-        guard = kept("guard", [P, 1], F32)
-        one = kept("one", [P, 1], F32)
+        wa_sc = sbuf("wa_sc", [P, 2, E], U8)
+        wctx_sc = sbuf("wctx_sc", [P, 1, E], U8)
+        wz_sc = sbuf("wz_sc", [P, 1, C], U8)
+        ident = sbuf("ident", [P, P], F32)
+        zeros = sbuf("zeros", [P, C], BF16)
+        guard = sbuf("guard", [P, 1], F32)
+        half_one = sbuf("half_one", [P, 1], F32)
         nc.gpsimd.memset(wa_sc[:].bitcast(I32), 0)
         make_identity(nc, ident[:])
         nc.gpsimd.memset(wctx_sc[:].bitcast(I32), 0)
         nc.gpsimd.memset(wz_sc[:].bitcast(I32), 0)
-        nc.vector.memset(warm[:], 0.0)
         nc.vector.memset(zeros[:].bitcast(I32), 0)
         nc.vector.memset(guard[:], LN_GUARD)
-        nc.vector.memset(one[:], 1.0)
 
         def load_scales(queue, plane, scales):
             rows = scales.bitcast(I32).rearrange("g (q r) n -> r q g n", r=4)
             for r in range(4):
                 queue.dma_start(out=plane[r:P:32].bitcast(I32), in_=rows[r])
 
-        def load_words(name, words, half):
-            passes = words.shape[0]
-            tile = kept(name, [P, passes, C], U32)
-            src = words.rearrange("g p n t -> p g (n t)")[:, :, 4 * C * half : 4 * C * (half + 1)]
+        def load_words(name, words, first_column):
+            tile = sbuf(name, [P, words.shape[0], C], U32)
+            src = words.rearrange("g p n t -> p g (n t)")[:, :, PACK * first_column : PACK * (first_column + C)]
             nc.sync.dma_start(out=tile[:].bitcast(I32), in_=src.bitcast(I32))
             return tile
 
         def load_rows(name, rows, first, count, dtype):
-            tile = kept(name, [P, count, rows.shape[2]], dtype)
+            tile = sbuf("%s%d" % (name, first), [P, count, rows.shape[2]], dtype)
             nc.sync.dma_start(out=tile[:], in_=rows[:, first : first + count, :])
             return [tile[:, n, :] for n in range(count)]
 
         load_scales(nc.scalar, wa_sc, wa_scales)
-        nc.scalar.activation(out=warm_out[:], in_=warm[:], func=ACT.Sigmoid)
+        nc.scalar.activation(out=half_one[:], in_=zeros[:, 0:1], func=ACT.Sigmoid)
 
-        xs = kept("xs", [P, TILES * 8], F32)
+        u1_rows, u2_rows = u_rows[:, :, 0:C], u_rows[:, :, C:E]
+        xs = sbuf("xs", [P, TILES * SCALES_PER_ROW], F32)
         nc.sync.dma_start(out=xs[:], in_=x_scale.rearrange("(p i) j -> p (i j)", i=TILES))
-        xraw = load_rows("xraw0", x_rows, 0, 1, U8)
-        xraw = xraw + load_rows("xraw1", x_rows, 1, 1, U8)
-        xraw = xraw + load_rows("xraw2", x_rows, 2, 2, U8)
+        x_raw = load_rows("x_raw", x_rows, 0, 1, U8)
+        x_raw = x_raw + load_rows("x_raw", x_rows, 1, 1, U8)
+        x_raw = x_raw + load_rows("x_raw", x_rows, 2, 2, U8)
         wa1 = load_words("wa1", wa_words, 0)
-        xraw = xraw + load_rows("xraw4", x_rows, 4, 2, U8)
-        u1 = load_rows("u1a", u_rows[:, :, 0:C], 0, 2, BF16)
-        g4 = kept("g4", [P, 4], BF16)
-        nc.sync.dma_start(out=g4[:], in_=g.rearrange("(p t) -> p t", t=4))
-        xraw = xraw + load_rows("xraw6", x_rows, 6, 2, U8)
-        u1 = u1 + load_rows("u1b", u_rows[:, :, 0:C], 2, 2, BF16)
+        x_raw = x_raw + load_rows("x_raw", x_rows, 4, 2, U8)
+        u1 = load_rows("u1_", u1_rows, 0, 2, BF16)
+        g4 = sbuf("g4", [P, PACK], BF16)
+        nc.sync.dma_start(out=g4[:], in_=g.rearrange("(p t) -> p t", t=PACK))
+        x_raw = x_raw + load_rows("x_raw", x_rows, 6, 2, U8)
+        u1 = u1 + load_rows("u1_", u1_rows, 2, 2, BF16)
         load_scales(nc.sync, wctx_sc, wctx_scales)
-        wsc = load_words("wsc", wctx_words, 1)
-        u1 = u1 + load_rows("u1c", u_rows[:, :, 0:C], 4, 4, BF16)
-        zraw = load_rows("zrawa", z_rows, 0, 4, BF16)
-        zraw = zraw + load_rows("zrawb", z_rows, 4, 4, BF16)
+        wctx_v = load_words("wctx_v", wctx_words, C)
+        u1 = u1 + load_rows("u1_", u1_rows, 4, 4, BF16)
+        z_raw = load_rows("z_raw", z_rows, 0, 4, BF16) + load_rows("z_raw", z_rows, 4, 4, BF16)
         load_scales(nc.sync, wz_sc, wz_scales)
         wz = load_words("wz", wz_words, 0)
-        wa2 = load_words("wa2", wa_words, 1)
-        wmu = load_words("wmu", wctx_words, 0)
-        u2 = load_rows("u2a", u_rows[:, :, C:E], 0, 4, BF16)
-        u2 = u2 + load_rows("u2b", u_rows[:, :, C:E], 4, 4, BF16)
+        wa2 = load_words("wa2", wa_words, C)
+        wctx_mu = load_words("wctx_mu", wctx_words, 0)
+        u2 = load_rows("u2_", u2_rows, 0, 4, BF16) + load_rows("u2_", u2_rows, 4, 4, BF16)
 
-        nxs = kept("nxs", [P, TILES * 8], F32)
-        nc.vector.tensor_scalar(out=nxs[:], in0=xs[:], scalar1=-1.0, scalar2=None, op0=ALU.mult)
-        gx = kept("gx", [P, P, 4], BF16)
+        neg_xs = sbuf("neg_xs", [P, TILES * SCALES_PER_ROW], F32)
+        nc.vector.tensor_scalar(out=neg_xs[:], in0=xs[:], scalar1=-1.0, scalar2=None, op0=ALU.mult)
 
-        xcode = [kept("xcode%d" % i, [P, 2, P], U32) for i in range(TILES)]
-        xsc = [kept("xsc%d" % i, [P, 2, P], U8) for i in range(TILES)]
-        ycode = [kept("ycode%d" % i, [P, P], U32) for i in range(TILES)]
-        ysc = [kept("ysc%d" % i, [P, P], U8) for i in range(TILES)]
-        zcode = [kept("zcode%d" % j, [P, 2, P], U32) for j in range(PAIRS)]
-        zsc = [kept("zsc%d" % j, [P, 2, P], U8) for j in range(PAIRS)]
-        sg = [kept("sg%d" % j, [P, 2 * C], F32) for j in range(PAIRS)]
-        nsp = [kept("nsp%d" % j, [P, 2 * C], F32) for j in range(PAIRS)]
-        dl = [kept("dl%d" % j, [P, 2 * C], F32) for j in range(PAIRS)]
-        mm = [kept("mm%d" % j, [P, 4 * C], F32) for j in range(PAIRS)]
-        pp = sg
-        t = {}
+        g_wide = sbuf("g_wide", [P, P, PACK], BF16)
+        x_wide = each("x_wide", TILES, [P, D], BF16)
+        x_laid = each("x_laid", TILES, [P, D], BF16)
+        x_code, x_sc = each("x_code", TILES, [P, 2, P], U32), each("x_sc", TILES, [P, 2, P], U8)
+        y1 = each("y1_", TILES, [P, PACK, P], F32)
+        yg = each("yg", TILES, [P, P, PACK], BF16)
+        y_code, y_sc = each("y_code", TILES, [P, P], U32), each("y_sc", TILES, [P, P], U8)
+        z_laid = each("z_laid", PAIRS, [P, 2 * H], BF16)
+        z_code, z_sc = each("z_code", PAIRS, [P, 2, P], U32), each("z_sc", PAIRS, [P, 2, P], U8)
+        sig_ln_p = each("sig_ln_p", PAIRS, [P, 2 * C], F32)
+        sp_r = each("sp_r", PAIRS, [P, 2 * C], F32)
+        d_out = each("d_out", PAIRS, [P, 2 * C], F32)
+        edges = each("edges", PAIRS, [P, 2, 2 * C], F32)
+        in_bank = {}
+        v_at = {}
 
-        def half(tiles, i):
-            return tiles[i // 2][:, C * (i % 2) : C * (i % 2 + 1)]
+        def of_tile(pair_tiles, i):
+            return pair_tiles[i // 2][:, C * (i % 2) : C * (i % 2 + 1)]
 
-        def pieces(i):
-            return [slice(0, C)] if i < TILES - 1 else [slice(0, C // 2), slice(C // 2, C)]
-
-        def copy(eng, dst, src):
-            if eng == "A":
+        def copy(engine, dst, src):
+            if engine == "S":
                 nc.scalar.copy(out=dst, in_=src)
             else:
                 nc.vector.tensor_copy(out=dst, in_=src)
 
-        def widen(i, g_pass, eng):
-            if ("xb", i) not in t:
-                t["xb", i] = rotating("xb", [P, D], BF16)
-            for j in range(4 * g_pass, 4 * g_pass + 4):
-                cols = slice(BLK * j, BLK * (j + 1))
-                src = xraw[i][:, cols].bitcast(FP8)
-                s = nxs[:, 8 * i + j : 8 * i + j + 1]
-                if eng == "A":
-                    nc.scalar.activation(out=t["xb", i][:, cols], in_=src, func=ACT.Copy, scale=s)
+        def mx(acc, codes, scales, w_codes, w_scales, start, stop):
+            nc.tensor.matmul_mx(
+                out=acc,
+                lhsT=codes.bitcast(FP8X4),
+                lhsT_scale=scales,
+                rhs=w_codes.bitcast(FP8X4),
+                rhs_scale=w_scales,
+                start=start,
+                stop=stop,
+            )
+
+        def quantize(codes, scales, values):
+            nc.vector.quantize_mx(out=codes.bitcast(FP8X4), scales=scales, in_=values)
+
+        def warm(count):
+            if "warm" not in in_bank:
+                in_bank["warm"] = bank(WARM_BANK, [P, C])
+            for n in range(count):
+                nc.tensor.matmul(in_bank["warm"][:], lhsT=zeros[:, 0:P], rhs=zeros[:], start=True, stop=True)
+
+        def widen(i, g_pass, engine):
+            spans = K_PASS // SCALE_SPAN
+            for j in range(spans * g_pass, spans * (g_pass + 1)):
+                cols = slice(SCALE_SPAN * j, SCALE_SPAN * (j + 1))
+                src = x_raw[i][:, cols].bitcast(FP8)
+                scale = neg_xs[:, SCALES_PER_ROW * i + j : SCALES_PER_ROW * i + j + 1]
+                if engine == "S":
+                    nc.scalar.activation(out=x_wide[i][:, cols], in_=src, func=ACT.Copy, scale=scale)
                 else:
-                    nc.vector.tensor_scalar(out=t["xb", i][:, cols], in0=src, scalar1=s, scalar2=None, op0=ALU.mult)
+                    nc.vector.tensor_scalar(out=x_wide[i][:, cols], in0=src, scalar1=scale, scalar2=None, op0=ALU.mult)
 
-        def turn(dst, rows):
-            words = rows.bitcast(F32)
-            for w in (0, 1):
-                nc.tensor.transpose(dst[:, w, :], words[:, w : 256 : 2], ident[:])
+        def turn_words(acc, two_passes):
+            for n, rows in enumerate(two_passes):
+                words = rows.bitcast(F32)
+                for w in (0, 1):
+                    nc.tensor.transpose(acc[:, n, w, :], words[:, w : K_PASS // 2 : 2], ident[:])
 
-        def mx(acc, lc, ls, rc, rs, start, stop):
-            nc.tensor.matmul_mx(out=acc, lhsT=lc.bitcast(FP8X4), lhsT_scale=ls, rhs=rc.bitcast(FP8X4), rhs_scale=rs, start=start, stop=stop)
+        def lay_words(engine, laid, acc):
+            dst = laid[:].bitcast(F32).rearrange("p (n r w) -> p n r w", n=2, w=2)
+            copy(engine, dst, acc[:].rearrange("p n w r -> p n r w"))
 
-        def step(st, i, arg):
-            if st == "W":
-                if "warm" not in t:
-                    t["warm"] = bank(7, [P, C])
-                for n in range(i):
-                    nc.tensor.matmul(t["warm"][:], lhsT=zeros[:, 0:P], rhs=zeros[:], start=True, stop=True)
-            elif st == "GX":
-                nc.vector.tensor_copy(out=gx[:], in_=g4[:].unsqueeze(1).to_broadcast([P, P, 4]))
-            elif st == "XA":
-                widen(i, 0, arg)
-            elif st == "XB":
-                widen(i, 1, arg)
-            elif st == "XT":
-                t["pA", i] = bank(int(arg), [P, 2, 2, P])
-                for gp in (0, 1):
-                    turn(t["pA", i][:, gp], t["xb", i][:, 512 * gp : 512 * (gp + 1)])
-            elif st == "XC":
-                t["xg", i] = rotating("xg", [P, D], BF16)
-                copy(arg, t["xg", i][:].bitcast(F32).rearrange("p (g r w) -> p g r w", g=2, w=2), t["pA", i][:].rearrange("p g w r -> p g r w"))
-            elif st == "XQ":
-                nc.vector.quantize_mx(out=xcode[i][:].rearrange("p g r -> p (g r)").bitcast(FP8X4), scales=xsc[i][:].rearrange("p g r -> p (g r)"), in_=t["xg", i][:])
-            elif st == "Y1":
-                t["pB", i] = bank(int(arg), [P, C])
-                for gp in (0, 1):
-                    mx(t["pB", i][:], xcode[i][:, gp, :], xsc[i][:, gp, :], wa1[:, gp, :], wa_sc[:, gp, 0:C], gp == 0, gp == 1)
-            elif st == "E1":
-                t["y1", i] = rotating("y1", [P, 4, P], F32)
-                nc.vector.tensor_tensor(out=t["y1", i][:], in0=u1[i].rearrange("p (m t) -> p t m", t=4), in1=t["pB", i][:].rearrange("p (m t) -> p t m", t=4), op=ALU.subtract)
-            elif st == "YT":
-                t["pC", i] = bank(int(arg), [P, 4, P])
-                for k in range(4):
-                    nc.tensor.transpose(t["pC", i][:, k, :], t["y1", i][:, k, :], ident[:])
-            elif st == "E2":
-                t["yg", i] = rotating("yg", [P, P, 4], BF16)
-                nc.vector.tensor_tensor(out=t["yg", i][:], in0=t["pC", i][:].rearrange("p t r -> p r t"), in1=gx[:], op=ALU.mult)
-            elif st == "YQ":
-                nc.vector.quantize_mx(out=ycode[i][:].bitcast(FP8X4), scales=ysc[i][:], in_=t["yg", i][:].rearrange("p r t -> p (r t)"))
-            elif st == "KC":
-                t["pV", i] = bank(int(arg), [P, C])
-                t["v", i] = t["pV", i]
-                mx(t["pV", i][:], ycode[i][:], ysc[i][:], wsc[:, 0, :], wctx_sc[:, 0, C:E], True, True)
-            elif st == "SG":
-                nc.scalar.activation(out=half(sg, i), in_=t["pV", i][:], func=ACT.Sigmoid, scale=-1.0)
-            elif st == "VE":
-                t["v", i] = kept("vs%d" % i, [P, C], F32)
-                copy(arg, t["v", i][:], t["pV", i][:])
-            elif st == "ZT":
-                t["pZ", i] = bank(int(arg), [P, 2, 2, P])
-                for n in (0, 1):
-                    turn(t["pZ", i][:, n], zraw[2 * i + n])
-            elif st == "ZC":
-                t["zg", i] = rotating("zg", [P, D], BF16, 4)
-                copy(arg, t["zg", i][:].bitcast(F32).rearrange("p (g r w) -> p g r w", g=2, w=2), t["pZ", i][:].rearrange("p g w r -> p g r w"))
-            elif st == "ZQ":
-                nc.vector.quantize_mx(out=zcode[i][:].rearrange("p g r -> p (g r)").bitcast(FP8X4), scales=zsc[i][:].rearrange("p g r -> p (g r)"), in_=t["zg", i][:])
-            elif st == "D":
-                t["pD", i] = bank(int(arg), [P, C])
-                acc = t["pD", i][:]
-                for gp in (0, 1):
-                    mx(acc, xcode[i][:, gp, :], xsc[i][:, gp, :], wa2[:, gp, :], wa_sc[:, gp, C:E], gp == 0, False)
-                mx(acc, ycode[i][:], ysc[i][:], wmu[:, 0, :], wctx_sc[:, 0, 0:C], False, False)
-                mx(acc, zcode[i // 2][:, i % 2, :], zsc[i // 2][:, i % 2, :], wz[:, 0, :], wz_sc[:, 0, :], False, True)
-            elif st == "DE":
-                nc.vector.tensor_tensor(out=half(dl, i), in0=t["pD", i][:], in1=u2[i], op=ALU.subtract)
-            elif st == "AB":
-                if arg == "A":
-                    nc.scalar.activation(out=dl[i][:], in_=dl[i][:], func=ACT.Abs)
-                else:
-                    nc.vector.scalar_tensor_tensor(out=dl[i][:], in0=dl[i][:], scalar=-1.0, in1=dl[i][:], op0=ALU.mult, op1=ALU.max)
-            elif st == "LA":
-                nc.scalar.activation(out=sg[i][:], in_=sg[i][:], func=ACT.Ln, bias=guard[:])
-            elif st == "MN":
-                nc.vector.scalar_tensor_tensor(out=half(nsp, i), in0=t["v", i][:], scalar=-1.0, in1=half(sg, i), op0=ALU.mult, op1=ALU.min)
-            elif st == "LB":
-                nc.scalar.activation(out=nsp[i][:], in_=nsp[i][:], func=ACT.Ln, scale=-1.0 / 0.3, bias=one[:])
-            elif st == "H":
-                nc.scalar.activation(out=nsp[i][:], in_=nsp[i][:], func=ACT.Sigmoid, scale=-1.0)
-            elif st == "M1":
-                nc.vector.scalar_tensor_tensor(out=mm[i][:, 0 : 2 * C], in0=dl[i][:], scalar=-0.5, in1=nsp[i][:], op0=ALU.add, op1=ALU.mult)
-            elif st == "M2":
-                nc.vector.scalar_tensor_tensor(out=mm[i][:, 2 * C : 4 * C], in0=dl[i][:], scalar=0.5, in1=nsp[i][:], op0=ALU.add, op1=ALU.mult)
-            elif st == "SS":
-                nc.scalar.activation(out=mm[i][:], in_=mm[i][:], func=ACT.Sigmoid, scale=-1.0 / 0.15)
-            elif st == "P":
-                nc.vector.scalar_tensor_tensor(out=pp[i][:], in0=mm[i][:, 0 : 2 * C], scalar=P_FLOOR, in1=mm[i][:, 2 * C : 4 * C], op0=ALU.max, op1=ALU.subtract)
-            elif st == "LP":
-                for cols in pieces(i):
-                    nc.scalar.activation(out=half(pp, i)[:, cols], in_=half(pp, i)[:, cols], func=ACT.Ln, bias=guard[:])
-            elif st == "FN":
-                for cols in pieces(i):
-                    nc.vector.tensor_scalar(out=half(dl, i)[:, cols], in0=half(pp, i)[:, cols], scalar1=-1.0 / math.log(2.0), scalar2=-math.log(P_FLOOR) / math.log(2.0), op0=ALU.mult, op1=ALU.min)
-                    nc.sync.dma_start(out=out_rows[:, i, cols], in_=half(dl, i)[:, cols])
+        def flat(tile):
+            return tile[:].rearrange("p a b -> p (a b)")
 
-        for item in ORDER.split():
-            name, i, arg = item.split(".")
-            step(name, int(i), arg)
+        def turn_x(i, b):
+            in_bank["x", i] = bank(b, [P, 2, 2, P])
+            turn_words(in_bank["x", i], [x_wide[i][:, 0:K_PASS], x_wide[i][:, K_PASS:D]])
+
+        def mm_y1(i, b):
+            in_bank["y1", i] = bank(b, [P, C])
+            for n in (0, 1):
+                mx(in_bank["y1", i][:], x_code[i][:, n, :], x_sc[i][:, n, :], wa1[:, n, :], wa_sc[:, n, 0:C], n == 0, n == 1)
+
+        def add_u1(i):
+            nc.vector.tensor_tensor(
+                out=y1[i][:],
+                in0=u1[i].rearrange("p (m t) -> p t m", t=PACK),
+                in1=in_bank["y1", i][:].rearrange("p (m t) -> p t m", t=PACK),
+                op=ALU.subtract,
+            )
+
+        def turn_y1(i, b):
+            in_bank["y1t", i] = bank(b, [P, PACK, P])
+            for t in range(PACK):
+                nc.tensor.transpose(in_bank["y1t", i][:, t, :], y1[i][:, t, :], ident[:])
+
+        def spread_g():
+            nc.vector.tensor_copy(out=g_wide[:], in_=g4[:].unsqueeze(1).to_broadcast([P, P, PACK]))
+
+        def gain(i):
+            src = in_bank["y1t", i][:].rearrange("p t r -> p r t")
+            nc.vector.tensor_tensor(out=yg[i][:], in0=src, in1=g_wide[:], op=ALU.mult)
+
+        def mm_v(i, b):
+            in_bank["v", i] = bank(b, [P, C])
+            v_at[i] = in_bank["v", i]
+            mx(v_at[i][:], y_code[i][:], y_sc[i][:], wctx_v[:, 0, :], wctx_sc[:, 0, C:E], True, True)
+
+        def sig_v(i):
+            nc.scalar.activation(out=of_tile(sig_ln_p, i), in_=in_bank["v", i][:], func=ACT.Sigmoid, scale=-1.0)
+
+        def park_v(i, engine):
+            v_at[i] = sbuf("v_parked%d" % i, [P, C], F32)
+            copy(engine, v_at[i][:], in_bank["v", i][:])
+
+        def turn_z(j, b):
+            in_bank["z", j] = bank(b, [P, 2, 2, P])
+            turn_words(in_bank["z", j], [z_raw[2 * j], z_raw[2 * j + 1]])
+
+        def mm_diff(i, b):
+            in_bank["diff", i] = bank(b, [P, C])
+            acc = in_bank["diff", i][:]
+            for n in (0, 1):
+                mx(acc, x_code[i][:, n, :], x_sc[i][:, n, :], wa2[:, n, :], wa_sc[:, n, C:E], n == 0, False)
+            mx(acc, y_code[i][:], y_sc[i][:], wctx_mu[:, 0, :], wctx_sc[:, 0, 0:C], False, False)
+            j, n = divmod(i, 2)
+            mx(acc, z_code[j][:, n, :], z_sc[j][:, n, :], wz[:, 0, :], wz_sc[:, 0, :], False, True)
+
+        def sub_u2(i):
+            nc.vector.tensor_tensor(out=of_tile(d_out, i), in0=in_bank["diff", i][:], in1=u2[i], op=ALU.subtract)
+
+        def abs_d(j):
+            diff = d_out[j][:]
+            nc.vector.scalar_tensor_tensor(out=diff, in0=diff, scalar=-1.0, in1=diff, op0=ALU.mult, op1=ALU.max)
+
+        def ln_sig(j):
+            nc.scalar.activation(out=sig_ln_p[j][:], in_=sig_ln_p[j][:], func=ACT.Ln, bias=guard[:])
+
+        def pick_sp(i):
+            nc.vector.scalar_tensor_tensor(
+                out=of_tile(sp_r, i), in0=v_at[i][:], scalar=-1.0, in1=of_tile(sig_ln_p, i), op0=ALU.mult, op1=ALU.min
+            )
+
+        def ln_den(j):
+            nc.scalar.activation(out=sp_r[j][:], in_=sp_r[j][:], func=ACT.Ln, scale=-2.5, bias=half_one[:])
+
+        steps = {
+            "warm": warm,
+            "widen_lo": lambda i, engine: widen(i, 0, engine),
+            "widen_hi": lambda i, engine: widen(i, 1, engine),
+            "turn_x": turn_x,
+            "lay_x": lambda i, engine: lay_words(engine, x_laid[i], in_bank["x", i]),
+            "quant_x": lambda i: quantize(flat(x_code[i]), flat(x_sc[i]), x_laid[i][:]),
+            "mm_y1": mm_y1,
+            "add_u1": add_u1,
+            "turn_y1": turn_y1,
+            "spread_g": spread_g,
+            "gain": gain,
+            "quant_y": lambda i: quantize(y_code[i][:], y_sc[i][:], flat(yg[i])),
+            "mm_v": mm_v,
+            "sig_v": sig_v,
+            "park_v": park_v,
+            "turn_z": turn_z,
+            "lay_z": lambda j, engine: lay_words(engine, z_laid[j], in_bank["z", j]),
+            "quant_z": lambda j: quantize(flat(z_code[j]), flat(z_sc[j]), z_laid[j][:]),
+            "mm_diff": mm_diff,
+            "sub_u2": sub_u2,
+            "abs_d": abs_d,
+            "ln_sig": ln_sig,
+            "pick_sp": pick_sp,
+            "ln_den": ln_den,
+        }
+
+        warm(HEAD_WARMUPS)
+        for entry in (FIRST_SIGMOID_PHASE + FIRST_LN_PHASE).split():
+            fields = entry.split(":")
+            steps[fields[0]](*[int(n) for n in fields[1:2]], *fields[2:])
+
+        for j in range(PAIRS):
+            nc.scalar.activation(out=sp_r[j][:], in_=sp_r[j][:], func=ACT.Sigmoid, scale=-1.0)
+        for j in range(PAIRS):
+            for side, shift in enumerate((-0.5, 0.5)):
+                nc.vector.scalar_tensor_tensor(
+                    out=edges[j][:, side, :], in0=d_out[j][:], scalar=shift, in1=sp_r[j][:], op0=ALU.add, op1=ALU.mult
+                )
+            nc.scalar.activation(out=flat(edges[j]), in_=flat(edges[j]), func=ACT.Sigmoid, scale=-5.0)
+        for j in range(PAIRS):
+            nc.vector.scalar_tensor_tensor(
+                out=sig_ln_p[j][:],
+                in0=edges[j][:, 0, :],
+                scalar=P_FLOOR,
+                in1=edges[j][:, 1, :],
+                op0=ALU.max,
+                op1=ALU.subtract,
+            )
+
+        for i in range(TILES):
+            pieces = [slice(0, C)] if i < TILES - 1 else [slice(0, C // 2), slice(C // 2, C)]
+            for cols in pieces:
+                mass = of_tile(sig_ln_p, i)[:, cols]
+                nc.scalar.activation(out=mass, in_=mass, func=ACT.Ln, bias=guard[:])
+            for cols in pieces:
+                bits = of_tile(d_out, i)[:, cols]
+                nc.vector.tensor_scalar(
+                    out=bits,
+                    in0=of_tile(sig_ln_p, i)[:, cols],
+                    scalar1=-1.0 / math.log(2.0),
+                    scalar2=-math.log(P_FLOOR) / math.log(2.0),
+                    op0=ALU.mult,
+                    op1=ALU.min,
+                )
+                nc.sync.dma_start(out=out_rows[:, i, cols], in_=bits)

import math
from contextlib import ExitStack

import concourse.mybir as mybir
from concourse.masks import make_identity

T, D, C, H = 1024, 1024, 512, 512
E = 2 * C
FLOPS = 2 * T * (D * E + C * E + H * C)

F32 = mybir.dt.float32
BF16 = mybir.dt.bfloat16
U32 = mybir.dt.uint32
I32 = mybir.dt.int32
U8 = mybir.dt.uint8
FP8 = mybir.dt.float8_e4m3fn
FP8X4 = mybir.dt.float8_e4m3fn_x4
ALU = mybir.AluOpType
ACT = mybir.ActivationFunctionType

P = 128
PACK = 4
K_PASS = P * PACK
TILES = T // P
PAIRS = TILES // 2
SCALE_SPAN = 128
SCALES_PER_ROW = D // SCALE_SPAN
LN_GUARD = 2.0**-63
P_FLOOR = 1e-6
WARM_BANK = 7
HEAD_WARMUPS = 9

FIRST_SIGMOID_PHASE = """
widen_lo:0:S widen_hi:0:V widen_hi:1:V widen_lo:1:S turn_x:0:0 warm:1 widen_lo:2:V widen_hi:2:V turn_x:1:1
warm:1 lay_x:0:S widen_lo:3:V widen_hi:3:V turn_x:2:2 warm:1 lay_x:1:S quant_x:0 turn_x:3:3 quant_x:1
lay_x:2:S lay_x:3:S widen_hi:4:S quant_x:2 widen_hi:5:S mm_y1:0:4 widen_lo:4:V quant_x:3 mm_y1:1:5
widen_lo:5:S mm_y1:2:6 mm_y1:3:7 add_u1:0 add_u1:1 turn_y1:0:0 turn_y1:1:1 add_u1:2 spread_g gain:0 add_u1:3
turn_x:4:2 turn_x:5:3 gain:1 widen_lo:6:S widen_hi:6:S turn_y1:2:4 widen_hi:7:S turn_x:6:5 turn_y1:3:6
widen_lo:7:S turn_x:7:0 lay_x:4:S quant_y:0 lay_x:5:S lay_x:6:S gain:2 quant_y:1 quant_x:4 mm_v:0:7 mm_v:1:1
mm_y1:4:4 lay_x:7:S quant_y:2 quant_x:5 mm_y1:5:2 park_v:0:S gain:3 mm_v:2:3 quant_x:6 mm_y1:6:5 quant_y:3
mm_v:3:6 quant_x:7 add_u1:4 add_u1:5 add_u1:6 mm_y1:7:0 turn_y1:4:4 gain:4 turn_z:0:2 sig_v:0 turn_z:1:7
turn_y1:5:5 sig_v:1 add_u1:7 quant_y:4 gain:5 turn_y1:6:4 turn_z:2:0 park_v:1:S lay_z:0:S gain:6 lay_z:1:S
quant_y:5 quant_z:0 sig_v:2 turn_y1:7:1 lay_z:2:S turn_z:3:2 quant_y:6 gain:7 sig_v:3 mm_v:4:7 mm_v:5:5
lay_z:3:V quant_y:7 quant_z:1 quant_z:2 mm_v:6:4 quant_z:3 mm_diff:0:0 mm_v:7:1 sig_v:4 sig_v:5 sig_v:6
sig_v:7
"""
FIRST_LN_PHASE = """
mm_diff:1:2 sub_u2:0 sub_u2:1 abs_d:0 mm_diff:2:0 mm_diff:3:2 sub_u2:2 sub_u2:3 mm_diff:4:0 mm_diff:5:2
ln_sig:0 ln_sig:1 ln_sig:2 ln_sig:3 pick_sp:0 pick_sp:1 pick_sp:2 mm_diff:6:3 sub_u2:4 mm_diff:7:0
pick_sp:3 pick_sp:4 pick_sp:5 pick_sp:6 pick_sp:7 ln_den:0 ln_den:1 ln_den:2 ln_den:3
sub_u2:5 sub_u2:6 abs_d:1 sub_u2:7 abs_d:2 abs_d:3
"""


def tile_channelconditionalsliceratemap_d1p_kernel(
    tc, x_bytes, x_scale, wa_words, wa_scales, u, g, wctx_words, wctx_scales, z, wz_words, wz_scales, out
):
    nc = tc.nc
    x_rows = x_bytes.rearrange("(p i) k -> p i k", i=TILES)
    u_rows = u.rearrange("(p i) e -> p i e", i=TILES)
    z_rows = z.rearrange("(p i) k -> p i k", i=TILES)
    out_rows = out.rearrange("(p i) c -> p i c", i=TILES)

    with ExitStack() as ctx:
        pool = ctx.enter_context(tc.tile_pool(name="sbuf", bufs=1))
        psum = ctx.enter_context(tc.psum_pool(name="psum", bufs=1))
        ctx.enter_context(tc.manual_schedule())

        def sbuf(name, shape, dtype):
            return pool.tile(shape, dtype, name=name, align_bytes=64)

        def each(name, count, shape, dtype):
            return [sbuf("%s%d" % (name, n), shape, dtype) for n in range(count)]

        def bank(number, shape):
            return psum.tile(shape, F32, name="bank%s" % number)

        wa_sc = sbuf("wa_sc", [P, 2, E], U8)
        wctx_sc = sbuf("wctx_sc", [P, 1, E], U8)
        wz_sc = sbuf("wz_sc", [P, 1, C], U8)
        ident = sbuf("ident", [P, P], F32)
        zeros = sbuf("zeros", [P, C], BF16)
        guard = sbuf("guard", [P, 1], F32)
        half_one = sbuf("half_one", [P, 1], F32)
        nc.gpsimd.memset(wa_sc[:].bitcast(I32), 0)
        make_identity(nc, ident[:])
        nc.gpsimd.memset(wctx_sc[:].bitcast(I32), 0)
        nc.gpsimd.memset(wz_sc[:].bitcast(I32), 0)
        nc.vector.memset(zeros[:].bitcast(I32), 0)
        nc.vector.memset(guard[:], LN_GUARD)

        def load_scales(queue, plane, scales):
            rows = scales.bitcast(I32).rearrange("g (q r) n -> r q g n", r=4)
            for r in range(4):
                queue.dma_start(out=plane[r:P:32].bitcast(I32), in_=rows[r])

        def load_words(name, words, first_column):
            tile = sbuf(name, [P, words.shape[0], C], U32)
            src = words.rearrange("g p n t -> p g (n t)")[:, :, PACK * first_column : PACK * (first_column + C)]
            nc.sync.dma_start(out=tile[:].bitcast(I32), in_=src.bitcast(I32))
            return tile

        def load_rows(name, rows, first, count, dtype):
            tile = sbuf("%s%d" % (name, first), [P, count, rows.shape[2]], dtype)
            nc.sync.dma_start(out=tile[:], in_=rows[:, first : first + count, :])
            return [tile[:, n, :] for n in range(count)]

        load_scales(nc.scalar, wa_sc, wa_scales)
        nc.scalar.activation(out=half_one[:], in_=zeros[:, 0:1], func=ACT.Sigmoid)

        u1_rows, u2_rows = u_rows[:, :, 0:C], u_rows[:, :, C:E]
        xs = sbuf("xs", [P, TILES * SCALES_PER_ROW], F32)
        nc.sync.dma_start(out=xs[:], in_=x_scale.rearrange("(p i) j -> p (i j)", i=TILES))
        x_raw = load_rows("x_raw", x_rows, 0, 1, U8)
        x_raw = x_raw + load_rows("x_raw", x_rows, 1, 1, U8)
        x_raw = x_raw + load_rows("x_raw", x_rows, 2, 2, U8)
        wa1 = load_words("wa1", wa_words, 0)
        x_raw = x_raw + load_rows("x_raw", x_rows, 4, 2, U8)
        u1 = load_rows("u1_", u1_rows, 0, 2, BF16)
        g4 = sbuf("g4", [P, PACK], BF16)
        nc.sync.dma_start(out=g4[:], in_=g.rearrange("(p t) -> p t", t=PACK))
        x_raw = x_raw + load_rows("x_raw", x_rows, 6, 2, U8)
        u1 = u1 + load_rows("u1_", u1_rows, 2, 2, BF16)
        load_scales(nc.sync, wctx_sc, wctx_scales)
        wctx_v = load_words("wctx_v", wctx_words, C)
        u1 = u1 + load_rows("u1_", u1_rows, 4, 4, BF16)
        z_raw = load_rows("z_raw", z_rows, 0, 4, BF16) + load_rows("z_raw", z_rows, 4, 4, BF16)
        load_scales(nc.sync, wz_sc, wz_scales)
        wz = load_words("wz", wz_words, 0)
        wa2 = load_words("wa2", wa_words, C)
        wctx_mu = load_words("wctx_mu", wctx_words, 0)
        u2 = load_rows("u2_", u2_rows, 0, 4, BF16) + load_rows("u2_", u2_rows, 4, 4, BF16)

        neg_xs = sbuf("neg_xs", [P, TILES * SCALES_PER_ROW], F32)
        nc.vector.tensor_scalar(out=neg_xs[:], in0=xs[:], scalar1=-1.0, scalar2=None, op0=ALU.mult)

        g_wide = sbuf("g_wide", [P, P, PACK], BF16)
        x_wide = each("x_wide", TILES, [P, D], BF16)
        x_laid = each("x_laid", TILES, [P, D], BF16)
        x_code, x_sc = each("x_code", TILES, [P, 2, P], U32), each("x_sc", TILES, [P, 2, P], U8)
        y1 = each("y1_", TILES, [P, PACK, P], F32)
        yg = each("yg", TILES, [P, P, PACK], BF16)
        y_code, y_sc = each("y_code", TILES, [P, P], U32), each("y_sc", TILES, [P, P], U8)
        z_laid = each("z_laid", PAIRS, [P, 2 * H], BF16)
        z_code, z_sc = each("z_code", PAIRS, [P, 2, P], U32), each("z_sc", PAIRS, [P, 2, P], U8)
        sig_ln_p = each("sig_ln_p", PAIRS, [P, 2 * C], F32)
        sp_r = each("sp_r", PAIRS, [P, 2 * C], F32)
        d_out = each("d_out", PAIRS, [P, 2 * C], F32)
        edges = each("edges", PAIRS, [P, 2, 2 * C], F32)
        in_bank = {}
        v_at = {}

        def of_tile(pair_tiles, i):
            return pair_tiles[i // 2][:, C * (i % 2) : C * (i % 2 + 1)]

        def copy(engine, dst, src):
            if engine == "S":
                nc.scalar.copy(out=dst, in_=src)
            else:
                nc.vector.tensor_copy(out=dst, in_=src)

        def mx(acc, codes, scales, w_codes, w_scales, start, stop):
            nc.tensor.matmul_mx(
                out=acc,
                lhsT=codes.bitcast(FP8X4),
                lhsT_scale=scales,
                rhs=w_codes.bitcast(FP8X4),
                rhs_scale=w_scales,
                start=start,
                stop=stop,
            )

        def quantize(codes, scales, values):
            nc.vector.quantize_mx(out=codes.bitcast(FP8X4), scales=scales, in_=values)

        def warm(count):
            if "warm" not in in_bank:
                in_bank["warm"] = bank(WARM_BANK, [P, C])
            for n in range(count):
                nc.tensor.matmul(in_bank["warm"][:], lhsT=zeros[:, 0:P], rhs=zeros[:], start=True, stop=True)

        def widen(i, g_pass, engine):
            spans = K_PASS // SCALE_SPAN
            for j in range(spans * g_pass, spans * (g_pass + 1)):
                cols = slice(SCALE_SPAN * j, SCALE_SPAN * (j + 1))
                src = x_raw[i][:, cols].bitcast(FP8)
                scale = neg_xs[:, SCALES_PER_ROW * i + j : SCALES_PER_ROW * i + j + 1]
                if engine == "S":
                    nc.scalar.activation(out=x_wide[i][:, cols], in_=src, func=ACT.Copy, scale=scale)
                else:
                    nc.vector.tensor_scalar(out=x_wide[i][:, cols], in0=src, scalar1=scale, scalar2=None, op0=ALU.mult)

        def turn_words(acc, two_passes):
            for n, rows in enumerate(two_passes):
                words = rows.bitcast(F32)
                for w in (0, 1):
                    nc.tensor.transpose(acc[:, n, w, :], words[:, w : K_PASS // 2 : 2], ident[:])

        def lay_words(engine, laid, acc):
            dst = laid[:].bitcast(F32).rearrange("p (n r w) -> p n r w", n=2, w=2)
            copy(engine, dst, acc[:].rearrange("p n w r -> p n r w"))

        def flat(tile):
            return tile[:].rearrange("p a b -> p (a b)")

        def turn_x(i, b):
            in_bank["x", i] = bank(b, [P, 2, 2, P])
            turn_words(in_bank["x", i], [x_wide[i][:, 0:K_PASS], x_wide[i][:, K_PASS:D]])

        def mm_y1(i, b):
            in_bank["y1", i] = bank(b, [P, C])
            for n in (0, 1):
                mx(in_bank["y1", i][:], x_code[i][:, n, :], x_sc[i][:, n, :], wa1[:, n, :], wa_sc[:, n, 0:C], n == 0, n == 1)

        def add_u1(i):
            nc.vector.tensor_tensor(
                out=y1[i][:],
                in0=u1[i].rearrange("p (m t) -> p t m", t=PACK),
                in1=in_bank["y1", i][:].rearrange("p (m t) -> p t m", t=PACK),
                op=ALU.subtract,
            )

        def turn_y1(i, b):
            in_bank["y1t", i] = bank(b, [P, PACK, P])
            for t in range(PACK):
                nc.tensor.transpose(in_bank["y1t", i][:, t, :], y1[i][:, t, :], ident[:])

        def spread_g():
            nc.vector.tensor_copy(out=g_wide[:], in_=g4[:].unsqueeze(1).to_broadcast([P, P, PACK]))

        def gain(i):
            src = in_bank["y1t", i][:].rearrange("p t r -> p r t")
            nc.vector.tensor_tensor(out=yg[i][:], in0=src, in1=g_wide[:], op=ALU.mult)

        def mm_v(i, b):
            in_bank["v", i] = bank(b, [P, C])
            v_at[i] = in_bank["v", i]
            mx(v_at[i][:], y_code[i][:], y_sc[i][:], wctx_v[:, 0, :], wctx_sc[:, 0, C:E], True, True)

        def sig_v(i):
            nc.scalar.activation(out=of_tile(sig_ln_p, i), in_=in_bank["v", i][:], func=ACT.Sigmoid, scale=-1.0)

        def park_v(i, engine):
            v_at[i] = sbuf("v_parked%d" % i, [P, C], F32)
            copy(engine, v_at[i][:], in_bank["v", i][:])

        def turn_z(j, b):
            in_bank["z", j] = bank(b, [P, 2, 2, P])
            turn_words(in_bank["z", j], [z_raw[2 * j], z_raw[2 * j + 1]])

        def mm_diff(i, b):
            in_bank["diff", i] = bank(b, [P, C])
            acc = in_bank["diff", i][:]
            for n in (0, 1):
                mx(acc, x_code[i][:, n, :], x_sc[i][:, n, :], wa2[:, n, :], wa_sc[:, n, C:E], n == 0, False)
            mx(acc, y_code[i][:], y_sc[i][:], wctx_mu[:, 0, :], wctx_sc[:, 0, 0:C], False, False)
            j, n = divmod(i, 2)
            mx(acc, z_code[j][:, n, :], z_sc[j][:, n, :], wz[:, 0, :], wz_sc[:, 0, :], False, True)

        def sub_u2(i):
            nc.vector.tensor_tensor(out=of_tile(d_out, i), in0=in_bank["diff", i][:], in1=u2[i], op=ALU.subtract)

        def abs_d(j):
            diff = d_out[j][:]
            nc.vector.scalar_tensor_tensor(out=diff, in0=diff, scalar=-1.0, in1=diff, op0=ALU.mult, op1=ALU.max)

        def ln_sig(j):
            nc.scalar.activation(out=sig_ln_p[j][:], in_=sig_ln_p[j][:], func=ACT.Ln, bias=guard[:])

        def pick_sp(i):
            nc.vector.scalar_tensor_tensor(
                out=of_tile(sp_r, i), in0=v_at[i][:], scalar=-1.0, in1=of_tile(sig_ln_p, i), op0=ALU.mult, op1=ALU.min
            )

        def ln_den(j):
            nc.scalar.activation(out=sp_r[j][:], in_=sp_r[j][:], func=ACT.Ln, scale=-2.5, bias=half_one[:])

        steps = {
            "warm": warm,
            "widen_lo": lambda i, engine: widen(i, 0, engine),
            "widen_hi": lambda i, engine: widen(i, 1, engine),
            "turn_x": turn_x,
            "lay_x": lambda i, engine: lay_words(engine, x_laid[i], in_bank["x", i]),
            "quant_x": lambda i: quantize(flat(x_code[i]), flat(x_sc[i]), x_laid[i][:]),
            "mm_y1": mm_y1,
            "add_u1": add_u1,
            "turn_y1": turn_y1,
            "spread_g": spread_g,
            "gain": gain,
            "quant_y": lambda i: quantize(y_code[i][:], y_sc[i][:], flat(yg[i])),
            "mm_v": mm_v,
            "sig_v": sig_v,
            "park_v": park_v,
            "turn_z": turn_z,
            "lay_z": lambda j, engine: lay_words(engine, z_laid[j], in_bank["z", j]),
            "quant_z": lambda j: quantize(flat(z_code[j]), flat(z_sc[j]), z_laid[j][:]),
            "mm_diff": mm_diff,
            "sub_u2": sub_u2,
            "abs_d": abs_d,
            "ln_sig": ln_sig,
            "pick_sp": pick_sp,
            "ln_den": ln_den,
        }

        warm(HEAD_WARMUPS)
        for entry in (FIRST_SIGMOID_PHASE + FIRST_LN_PHASE).split():
            fields = entry.split(":")
            steps[fields[0]](*[int(n) for n in fields[1:2]], *fields[2:])

        for j in range(PAIRS):
            nc.scalar.activation(out=sp_r[j][:], in_=sp_r[j][:], func=ACT.Sigmoid, scale=-1.0)
        for j in range(PAIRS):
            for side, shift in enumerate((-0.5, 0.5)):
                nc.vector.scalar_tensor_tensor(
                    out=edges[j][:, side, :], in0=d_out[j][:], scalar=shift, in1=sp_r[j][:], op0=ALU.add, op1=ALU.mult
                )
            nc.scalar.activation(out=flat(edges[j]), in_=flat(edges[j]), func=ACT.Sigmoid, scale=-5.0)
        for j in range(PAIRS):
            nc.vector.scalar_tensor_tensor(
                out=sig_ln_p[j][:],
                in0=edges[j][:, 0, :],
                scalar=P_FLOOR,
                in1=edges[j][:, 1, :],
                op0=ALU.max,
                op1=ALU.subtract,
            )

        for i in range(TILES):
            pieces = [slice(0, C)] if i < TILES - 1 else [slice(0, C // 2), slice(C // 2, C)]
            for cols in pieces:
                mass = of_tile(sig_ln_p, i)[:, cols]
                nc.scalar.activation(out=mass, in_=mass, func=ACT.Ln, bias=guard[:])
            for cols in pieces:
                bits = of_tile(d_out, i)[:, cols]
                nc.vector.tensor_scalar(
                    out=bits,
                    in0=of_tile(sig_ln_p, i)[:, cols],
                    scalar1=-1.0 / math.log(2.0),
                    scalar2=-math.log(P_FLOOR) / math.log(2.0),
                    op0=ALU.mult,
                    op1=ALU.min,
                )
                nc.sync.dma_start(out=out_rows[:, i, cols], in_=bits)
